import numpy as np
import ml_dtypes


def mxq(x, axis, fmt="e4m3"):
    dtype, down = {"e4m3": (ml_dtypes.float8_e4m3fn, 7), "e5m2": (ml_dtypes.float8_e5m2, 14)}[fmt]
    v = np.moveaxis(np.asarray(x, np.float32).astype(ml_dtypes.bfloat16).astype(np.float64), axis, -1)
    blocks = v.reshape(v.shape[:-1] + (-1, 32))
    amax = np.abs(blocks).max(-1, keepdims=True)
    byte = np.maximum(np.where(amax > 0, np.frexp(amax)[1] - 1 + 127, 0) - down, 1)
    scale = np.exp2(byte - 127.0)
    codes = (blocks / scale).astype(np.float32).astype(dtype).astype(np.float64)
    return np.moveaxis((codes * scale).reshape(v.shape), -1, axis)


WIDE = False


def mx_kscale(k):
    if not WIDE:
        return np.ones(k)
    levels = np.array([10, -10, 5, -5, 0])
    if k % 512:
        return np.exp2(np.random.permutation(np.resize(levels, k // 32))).repeat(32)
    a = np.empty((k // 512, 16))
    for p in range(k // 512):
        a[p, :8] = np.random.permutation(np.resize(levels, 8))
        for g in range(8):
            far = levels[np.abs(levels - a[p, g]) >= 10]
            a[p, g + 8] = far[np.random.randint(len(far))]
    return np.exp2(a.ravel()).repeat(32)


def f64(x):
    return np.asarray(x).astype(np.float64)


def striped(idx):
    return np.tile(idx.reshape(-1, 16).T, (8, 1)).astype(np.uint16)


def unstriped(offs):
    return offs[:16].T.reshape(-1).astype(np.int64)


def pack_weight(w):
    k, n = w.shape
    w = f64(np.asarray(w, np.float32).astype(ml_dtypes.bfloat16)).reshape(k // 32, 32, n)
    amax = np.abs(w).max(1)
    byte = np.clip(np.where(amax > 0, np.frexp(amax)[1] - 1 + 127 - 7, 1), 1, 254)
    scaled = (w * np.exp2(127.0 - byte)[:, None, :]).reshape(k, n).astype(np.float32)
    words = np.ascontiguousarray(scaled.reshape(k // 512, 128, 4, n).transpose(0, 1, 3, 2)).astype(ml_dtypes.float8_e4m3fn).view(np.uint8)
    return words, np.ascontiguousarray(byte.astype(np.uint8).reshape(k // 512, 16, n))


def unpack_weight(words, scales):
    g, p, n, _ = words.shape
    vals = np.ascontiguousarray(words).view(ml_dtypes.float8_e4m3fn).astype(np.float64) * np.repeat(np.exp2(scales.astype(np.float64) - 127.0), 8, axis=1)[..., None]
    return vals.transpose(0, 1, 3, 2).reshape(g * 512, n)


def sigmoid(v):
    return 1.0 / (1.0 + np.exp(-np.maximum(v, -700.0)))


K, T, S, N, H = 1024, 1024, 512, 256, 512


def setup_inputs():
    n = np.random.standard_normal
    s = mx_kscale(K)[:, None]
    u = mx_kscale(H)
    packed_xT = pack_weight(n((K, T)) * s)
    return {
        "x_words": packed_xT[0],
        "x_scales": packed_xT[1],
        "w1": (n((K, H)) / np.sqrt(K) / s).astype(np.float32),
        "w2": (n((K, H)) / np.sqrt(K) / s).astype(np.float32),
        "w3": (n((K, H)) / np.sqrt(K) / s).astype(np.float32),
        "trt": (np.random.uniform(0.0, 1.0, (H, S))).astype(np.float32),
        "yy0": (n((H, S))).astype(np.float32),
        "unit": (np.random.uniform(0.6, 1.4, (H, 1)) * u[:, None]).astype(np.float32),
        "w4": (n((H, N)) / np.sqrt(H) / u[:, None]).astype(np.float32),
        "offs": striped(np.random.permutation(T)[:S]),
        "tw": striped(np.random.permutation(S)),
    }


def reference(x_words, x_scales, w1, w2, w3, trt, yy0, unit, w4, offs, tw):
    xq = unpack_weight(x_words, x_scales)[:, unstriped(offs)]
    m1 = mxq(f64(w2), 0, "e4m3").T @ xq
    m0 = mxq(f64(w1), 0, "e4m3").T @ xq
    pe = mxq(f64(w3), 0, "e4m3").T @ xq
    prop = 0.8 * sigmoid(pe) + 0.1
    clev = (f64(trt) - prop) / (prop * (-1.0 * prop + 1.0))
    resid = f64(yy0) - (f64(trt) * m1 + (-1.0 * f64(trt) + 1.0) * m0)
    tau = m1 - m0 + 0.3 * (clev * resid)
    tt = tau[:, unstriped(tw)]
    hid = f64(unit) * (tau - (0.5 * tt))
    return mxq(f64(w4), 0, "e4m3").T @ mxq(hid, 0, "e4m3")

@@ -1,0 +1,270 @@
+import math
+from contextlib import ExitStack
+
+import concourse.mybir as mybir
+
+K, T, S, N, H = 1024, 1024, 512, 256, 512
+FLOPS = 3 * 2 * K * H * S + 2 * H * N * S
+
+F32 = mybir.dt.float32
+BF16 = mybir.dt.bfloat16
+I32 = mybir.dt.int32
+U32 = mybir.dt.uint32
+U16 = mybir.dt.uint16
+U8 = mybir.dt.uint8
+FP8X4 = mybir.dt.float8_e4m3fn_x4
+ALU = mybir.AluOpType
+ACT = mybir.ActivationFunctionType
+
+P = 128
+PACK = 4
+PASSES = K // (P * PACK)
+HALF = S // 2
+LN3 = math.log(3.0)
+ALPHA = 1.25
+KAPPA = -0.3 * 40.0 / 9.0
+SPLIT_TILE = 0
+V_SHARE = 88
+
+
+def tile_picked_yuplif_dr_p_kernel(tc, x_words, x_scales, w1, w2, w3, trt, yy0, unit, w4, offs, tw, out):
+    nc = tc.nc
+    with ExitStack() as ctx:
+        keep = ctx.enter_context(tc.tile_pool(name="keep", bufs=1))
+        psum = ctx.enter_context(tc.psum_pool(name="psum", bufs=1))
+
+        def sb(name, shape, dtype, tag=None):
+            return keep.tile(shape, dtype, name=name, tag=tag or name, align_bytes=64)
+
+        offs_sb = keep.tile([P, S // 16], U16, name="offs_sb")
+        tw_sb = keep.tile([P, S // 16], U16, name="tw_sb")
+        x_table = [sb("x_table%d" % o, [P, T], U32) for o in range(PASSES)]
+        xs_table = sb("xs_table", [P, T], U8)
+        raw = {(n, o): sb("raw_%s_%d" % (n, o), [P, PACK, H], F32) for n in ("w1", "w2", "w3") for o in range(PASSES)}
+        w4_raw = sb("w4_raw", [P, PACK, N], F32)
+        trt_sb = sb("trt_sb", [P, PACK, S], F32)
+        yy_sb = sb("yy_sb", [P, PACK, S], F32)
+        unit_sb = sb("unit_sb", [P, PACK], F32)
+        weights = {"w1": w1, "w2": w2, "w3": w3}
+
+        def load_weight(n, o):
+            rows = weights[n][o * P * PACK : (o + 1) * P * PACK, :]
+            nc.sync.dma_start(out=raw[n, o][:], in_=rows.rearrange("(p j) c -> p j c", j=PACK))
+
+        def load_words(o):
+            nc.sync.dma_start(out=x_table[o][:].bitcast(I32), in_=x_words[o].rearrange("p n r -> p (n r)").bitcast(I32))
+
+        nc.gpsimd.memset(xs_table[:].bitcast(I32), 0)
+        nc.sync.dma_start(out=offs_sb[:], in_=offs)
+        load_words(0)
+        for q in range(4):
+            nc.sync.dma_start(
+                out=xs_table[32 * q : 32 * q + 4 * PASSES, :].bitcast(I32),
+                in_=x_scales[:, 4 * q : 4 * q + 4, :].bitcast(I32),
+            )
+        load_weight("w3", 0)
+        load_words(1)
+        load_weight("w3", 1)
+        nc.sync.dma_start(out=unit_sb[:], in_=unit.rearrange("(p t) o -> p (t o)", t=PACK))
+        nc.sync.dma_start(out=trt_sb[:], in_=trt.rearrange("(p t) j -> p t j", t=PACK))
+        load_weight("w1", 0)
+        load_weight("w1", 1)
+        nc.sync.dma_start(out=tw_sb[:], in_=tw)
+        nc.sync.dma_start(out=yy_sb[:], in_=yy0.rearrange("(p t) j -> p t j", t=PACK))
+        load_weight("w2", 0)
+        load_weight("w2", 1)
+        nc.sync.dma_start(out=w4_raw[:], in_=w4.rearrange("(p j) c -> p j c", j=PACK))
+
+        x_codes = [sb("x_codes%d" % o, [P, S], U32) for o in range(PASSES)]
+        x_sc = sb("x_sc", [P, S], U8)
+        grouped = {}
+        lodging = {("w3", 0): "stage", ("w3", 1): "stage", ("w1", 0): "stage", ("w1", 1): "up0", ("w2", 0): "up1", ("w2", 1): "stage"}
+
+        def stage(key):
+            grouped[key] = sb("grp_%s_%d" % key, [P, PACK * H], BF16, tag=lodging[key])
+
+        codes = {key: sb("codes_%s_%d" % key, [P, H], U32) for key in raw}
+        scales = {key: sb("scales_%s_%d" % key, [P, H], U8) for key in raw}
+
+        def views(key, m0, m1):
+            dst = grouped[key][:].rearrange("p (t m j) -> p m t j", t=PACK, j=PACK)[:, m0:m1]
+            src = raw[key][:].rearrange("p j (m t) -> p m t j", t=PACK)[:, m0:m1]
+            return dst, src
+
+        def round_on_scalar(key, m0, m1):
+            dst, src = views(key, m0, m1)
+            nc.scalar.activation(dst, src, ACT.Copy, scale=-1.0 if key[0] == "w1" else 1.0)
+
+        def quantize(key, t0, t1):
+            nc.vector.quantize_mx(
+                out=codes[key][:, t0 * P : t1 * P].bitcast(FP8X4),
+                scales=scales[key][:, t0 * P : t1 * P],
+                in_=grouped[key][:, t0 * H : t1 * H],
+            )
+
+        def product_pass(acc, n, o, t, start, stop):
+            cols = slice(t * P, (t + 1) * P)
+            nc.tensor.matmul_mx(
+                out=acc[:],
+                lhsT=codes[n, o][:, cols].bitcast(FP8X4),
+                lhsT_scale=scales[n, o][:, cols],
+                rhs=x_codes[o][:].bitcast(FP8X4),
+                rhs_scale=x_sc[4 * o :, :],
+                start=start,
+                stop=stop,
+            )
+
+        def rows(name):
+            return [sb("%s%d" % (name, t), [P, S], F32) for t in range(PACK)]
+
+        nc.vector.tensor_copy(x_codes[0][:], x_table[0][:].indirect(offs_sb[:]))
+        nc.vector.tensor_copy(x_sc[:], xs_table[:].indirect(offs_sb[:]))
+        stage(("w3", 0))
+        round_on_scalar(("w3", 0), 0, P)
+        nc.vector.tensor_copy(x_codes[1][:], x_table[1][:].indirect(offs_sb[:]))
+        quantize(("w3", 0), 0, PACK)
+        pe = [psum.tile([P, S], F32, name="pe%d" % t, tag="a%d" % t) for t in range(PACK)]
+        for t in range(PACK):
+            product_pass(pe[t], "w3", 0, t, True, False)
+        stage(("w3", 1))
+        dst, src = views(("w3", 1), 0, V_SHARE)
+        nc.vector.tensor_copy(dst, src)
+        round_on_scalar(("w3", 1), V_SHARE, P)
+        up = [sb("up%d" % g, [P, 2, S], F32) for g in range(2)]
+        down = [sb("down%d" % g, [P, 2, S], F32) for g in range(2)]
+        for t in range(PACK):
+            quantize(("w3", 1), t, t + 1)
+            product_pass(pe[t], "w3", 1, t, False, True)
+            nc.scalar.activation(up[t // 2][:, t % 2, :], pe[t][:], ACT.Tanh, bias=LN3, scale=0.5)
+            nc.scalar.activation(down[t // 2][:, t % 2, :], pe[t][:], ACT.Tanh, bias=-LN3, scale=0.5)
+
+        neg_m0 = [psum.tile([P, S], F32, name="neg_m0%d" % t, tag="b%d" % t) for t in range(PACK)]
+        diff = [psum.tile([P, S], F32, name="diff%d" % t, tag="a%d" % t) for t in range(PACK)]
+        ku = sb("ku", [P, PACK], F32)
+        nc.vector.tensor_scalar(ku[:], unit_sb[:], KAPPA, None, ALU.mult)
+        clev = [sb("clev%d" % g, [P, 2, S], F32) for g in range(2)]
+        ct, err, ce = rows("ct"), rows("err"), rows("ce")
+
+        def clev_rows(t):
+            return clev[t // 2][:, t % 2, :]
+
+        def clev_steps(dst, hi, lo, treat):
+            return [
+                lambda: nc.vector.tensor_tensor(hi, hi, lo, ALU.subtract),
+                lambda: nc.vector.scalar_tensor_tensor(hi, hi, -2.0 * ALPHA, treat, ALU.add, ALU.mult),
+                lambda: nc.vector.scalar_tensor_tensor(dst, lo, ALPHA, hi, ALU.add, ALU.add),
+            ]
+
+        def make_ct(t):
+            nc.vector.scalar_tensor_tensor(ct[t][:], clev_rows(t), ku[:, t : t + 1], trt_sb[:, t, :], ALU.mult, ALU.mult)
+
+        stage(("w1", 0))
+        round_on_scalar(("w1", 0), 0, P)
+        quantize(("w1", 0), 0, PACK)
+        for t in range(PACK):
+            product_pass(neg_m0[t], "w1", 0, t, True, False)
+
+        first = [clev_steps(clev[0][:, t, :], up[0][:, t, :], down[0][:, t, :], trt_sb[:, t, :]) for t in range(2)]
+        for k in range(3):
+            first[0][k]()
+            first[1][k]()
+
+        stage(("w1", 1))
+        round_on_scalar(("w1", 1), 0, P)
+        for t in range(PACK):
+            quantize(("w1", 1), t, t + 1)
+            product_pass(neg_m0[t], "w1", 1, t, False, True)
+        for t in range(PACK):
+            if t != SPLIT_TILE:
+                product_pass(diff[t], "w1", 0, t, True, False)
+                product_pass(diff[t], "w1", 1, t, False, False)
+
+        second = clev_steps(clev[1][:], up[1][:], down[1][:], trt_sb[:, 2:4, :])
+        second[0]()
+        make_ct(0)
+        second[1]()
+        make_ct(1)
+        second[2]()
+
+        stage(("w2", 0))
+        round_on_scalar(("w2", 0), 0, P)
+        quantize(("w2", 0), 0, PACK)
+        for t in range(PACK):
+            product_pass(diff[t], "w2", 0, t, t == SPLIT_TILE, False)
+        stage(("w2", 1))
+        round_on_scalar(("w2", 1), 0, P)
+        neg_m0_sb = sb("neg_m0_sb", [P, S], F32)
+        nc.scalar.activation(neg_m0_sb[:], neg_m0[SPLIT_TILE][:], ACT.Copy)
+        for t in range(PACK):
+            quantize(("w2", 1), t, t + 1)
+            product_pass(diff[t], "w2", 1, t, False, True)
+
+        w4_grouped = sb("w4_grouped", [P, PACK * N], BF16, tag="down0")
+        nc.scalar.activation(
+            w4_grouped[:].rearrange("p (c i j) -> p c j i", i=4, j=PACK),
+            w4_raw[:].rearrange("p j (c i) -> p c j i", i=4),
+            ACT.Copy,
+        )
+        w4_codes = sb("w4_codes", [P, N], U32)
+        w4_scales = sb("w4_scales", [P, N], U8)
+        nc.vector.quantize_mx(out=w4_codes[:].bitcast(FP8X4), scales=w4_scales[:], in_=w4_grouped[:])
+
+        make_ct(2)
+        make_ct(3)
+        for t in range(PACK):
+            nc.vector.tensor_tensor(err[t][:], neg_m0[t][:], yy_sb[:, t, :], ALU.add)
+        for t in range(PACK):
+            nc.vector.scalar_tensor_tensor(ce[t][:], clev_rows(t), ku[:, t : t + 1], err[t][:], ALU.mult, ALU.mult)
+
+        diff_sb = sb("diff_sb", [P, S], F32)
+        nc.vector.tensor_tensor(diff_sb[:], diff[SPLIT_TILE][:], neg_m0_sb[:], ALU.add)
+        dv = rows("dv")
+        tau = sb("tau", [P, PACK, S], F32)
+        twin = [sb("twin%d" % h, [P, PACK, HALF], F32) for h in range(2)]
+
+        def make_dv(t):
+            d = diff_sb if t == SPLIT_TILE else diff[t]
+            nc.vector.scalar_tensor_tensor(dv[t][:], ct[t][:], unit_sb[:, t : t + 1], d[:], ALU.subtract, ALU.mult)
+
+        make_dv(0)
+        for t in range(PACK):
+            if t + 1 < PACK:
+                make_dv(t + 1)
+            nc.vector.tensor_tensor(tau[:, t, :], ce[t][:], dv[t][:], ALU.subtract)
+            for h in range(2):
+                nc.scalar.activation(
+                    twin[h][:, t, :],
+                    tau[:, t, :].indirect(tw_sb[:, h * HALF // 16 : (h + 1) * HALF // 16]),
+                    ACT.Copy,
+                    scale=-0.5,
+                )
+
+        for h in range(2):
+            cols = slice(h * HALF, (h + 1) * HALF)
+            hid_grouped = sb("hid_grouped%d" % h, [P, PACK * HALF], BF16)
+            nc.vector.tensor_tensor(
+                hid_grouped[:].rearrange("p (c i t) -> p c t i", i=2, t=PACK),
+                tau[:, :, cols].rearrange("p t (c i) -> p c t i", i=2),
+                twin[h][:].rearrange("p t (c i) -> p c t i", i=2),
+                ALU.add,
+            )
+            hid_codes = sb("hid_codes%d" % h, [P, HALF], U32)
+            hid_scales = sb("hid_scales%d" % h, [P, HALF], U8)
+            nc.vector.quantize_mx(out=hid_codes[:].bitcast(FP8X4), scales=hid_scales[:], in_=hid_grouped[:])
+            for b in range(N // P):
+                acc = psum.tile([P, HALF], F32, name="acc%d%d" % (h, b), tag="b%d" % (2 * h + b))
+                nc.tensor.matmul_mx(
+                    out=acc[:],
+                    lhsT=w4_codes[:, b * P : (b + 1) * P].bitcast(FP8X4),
+                    lhsT_scale=w4_scales[:, b * P : (b + 1) * P],
+                    rhs=hid_codes[:].bitcast(FP8X4),
+                    rhs_scale=hid_scales[:],
+                    start=True,
+                    stop=True,
+                )
+                res = sb("res%d%d" % (h, b), [P, HALF], F32)
+                if h == 1 and b == 1:
+                    nc.vector.tensor_copy(res[:], acc[:])
+                else:
+                    nc.scalar.activation(res[:], acc[:], ACT.Copy)
+                nc.sync.dma_start(out=out[b * P : (b + 1) * P, cols], in_=res[:])

@@ -20,11 +20,11 @@ P = 128
 PACK = 4
 PASSES = K // (P * PACK)
 HALF = S // 2
+QUARTER = S // 4
 LN3 = math.log(3.0)
 ALPHA = 1.25
 KAPPA = -0.3 * 40.0 / 9.0
 SPLIT_TILE = 0
-V_SHARE = 88
 
 
 def tile_picked_yuplif_dr_p_kernel(tc, x_words, x_scales, w1, w2, w3, trt, yy0, unit, w4, offs, tw, out):
@@ -77,29 +77,26 @@ def tile_picked_yuplif_dr_p_kernel(tc, x_words, x_scales, w1, w2, w3, trt, yy0, 
 
         x_codes = [sb("x_codes%d" % o, [P, S], U32) for o in range(PASSES)]
         x_sc = sb("x_sc", [P, S], U8)
-        grouped = {}
-        lodging = {("w3", 0): "stage", ("w3", 1): "stage", ("w1", 0): "stage", ("w1", 1): "up0", ("w2", 0): "up1", ("w2", 1): "stage"}
-
-        def stage(key):
-            grouped[key] = sb("grp_%s_%d" % key, [P, PACK * H], BF16, tag=lodging[key])
-
         codes = {key: sb("codes_%s_%d" % key, [P, H], U32) for key in raw}
         scales = {key: sb("scales_%s_%d" % key, [P, H], U8) for key in raw}
+        grouped = {}
 
-        def views(key, m0, m1):
-            dst = grouped[key][:].rearrange("p (t m j) -> p m t j", t=PACK, j=PACK)[:, m0:m1]
-            src = raw[key][:].rearrange("p j (m t) -> p m t j", t=PACK)[:, m0:m1]
-            return dst, src
-
-        def round_on_scalar(key, m0, m1):
-            dst, src = views(key, m0, m1)
-            nc.scalar.activation(dst, src, ACT.Copy, scale=-1.0 if key[0] == "w1" else 1.0)
+        def round_pair(key, g, tag, engine="scalar"):
+            tile = sb("grp_%s_%d_%d" % (key + (g,)), [P, 2 * H], BF16, tag=tag)
+            grouped[key, g] = tile
+            dst = tile[:].rearrange("p (e m j) -> p m j e", e=2, j=PACK)
+            src = raw[key][:].rearrange("p j (m g e) -> p g m j e", g=2, e=2)[:, g]
+            if engine == "vector":
+                nc.vector.tensor_copy(dst, src)
+            else:
+                nc.scalar.activation(dst, src, ACT.Copy, scale=-1.0 if key[0] == "w1" else 1.0)
 
         def quantize(key, t0, t1):
+            e0 = t0 % 2
             nc.vector.quantize_mx(
                 out=codes[key][:, t0 * P : t1 * P].bitcast(FP8X4),
                 scales=scales[key][:, t0 * P : t1 * P],
-                in_=grouped[key][:, t0 * H : t1 * H],
+                in_=grouped[key, t0 // 2][:, e0 * H : (e0 + t1 - t0) * H],
             )
 
         def product_pass(acc, n, o, t, start, stop):
@@ -117,36 +114,39 @@ def tile_picked_yuplif_dr_p_kernel(tc, x_words, x_scales, w1, w2, w3, trt, yy0, 
         def rows(name):
             return [sb("%s%d" % (name, t), [P, S], F32) for t in range(PACK)]
 
+        def pairs(name):
+            return [sb("%s%d" % (name, g), [P, 2, S], F32) for g in range(2)]
+
+        def row(tiles, t):
+            return tiles[t // 2][:, t % 2, :]
+
+        def prepare(key, tags, acc, start, stop):
+            for g in range(2):
+                round_pair(key, g, tags[g])
+                quantize(key, 2 * g, 2 * g + 2)
+                for t in (2 * g, 2 * g + 1):
+                    product_pass(acc[t], key[0], key[1], t, start(t), stop)
+
         nc.vector.tensor_copy(x_codes[0][:], x_table[0][:].indirect(offs_sb[:]))
         nc.vector.tensor_copy(x_sc[:], xs_table[:].indirect(offs_sb[:]))
-        stage(("w3", 0))
-        round_on_scalar(("w3", 0), 0, P)
         nc.vector.tensor_copy(x_codes[1][:], x_table[1][:].indirect(offs_sb[:]))
-        quantize(("w3", 0), 0, PACK)
         pe = [psum.tile([P, S], F32, name="pe%d" % t, tag="a%d" % t) for t in range(PACK)]
-        for t in range(PACK):
-            product_pass(pe[t], "w3", 0, t, True, False)
-        stage(("w3", 1))
-        dst, src = views(("w3", 1), 0, V_SHARE)
-        nc.vector.tensor_copy(dst, src)
-        round_on_scalar(("w3", 1), V_SHARE, P)
-        up = [sb("up%d" % g, [P, 2, S], F32) for g in range(2)]
-        down = [sb("down%d" % g, [P, 2, S], F32) for g in range(2)]
+        prepare(("w3", 0), ("stage0", "stage1"), pe, lambda t: True, False)
+        round_pair(("w3", 1), 0, "stage0", "vector")
+        round_pair(("w3", 1), 1, "stage1")
+        up, down = pairs("up"), pairs("down")
         for t in range(PACK):
             quantize(("w3", 1), t, t + 1)
             product_pass(pe[t], "w3", 1, t, False, True)
-            nc.scalar.activation(up[t // 2][:, t % 2, :], pe[t][:], ACT.Tanh, bias=LN3, scale=0.5)
-            nc.scalar.activation(down[t // 2][:, t % 2, :], pe[t][:], ACT.Tanh, bias=-LN3, scale=0.5)
+            nc.scalar.activation(row(up, t), pe[t][:], ACT.Tanh, bias=LN3, scale=0.5)
+            nc.scalar.activation(row(down, t), pe[t][:], ACT.Tanh, bias=-LN3, scale=0.5)
 
         neg_m0 = [psum.tile([P, S], F32, name="neg_m0%d" % t, tag="b%d" % t) for t in range(PACK)]
         diff = [psum.tile([P, S], F32, name="diff%d" % t, tag="a%d" % t) for t in range(PACK)]
         ku = sb("ku", [P, PACK], F32)
         nc.vector.tensor_scalar(ku[:], unit_sb[:], KAPPA, None, ALU.mult)
-        clev = [sb("clev%d" % g, [P, 2, S], F32) for g in range(2)]
-        ct, err, ce = rows("ct"), rows("err"), rows("ce")
-
-        def clev_rows(t):
-            return clev[t // 2][:, t % 2, :]
+        clev, err = pairs("clev"), pairs("err")
+        ct = rows("ct")
 
         def clev_steps(dst, hi, lo, treat):
             return [
@@ -156,24 +156,16 @@ def tile_picked_yuplif_dr_p_kernel(tc, x_words, x_scales, w1, w2, w3, trt, yy0, 
             ]
 
         def make_ct(t):
-            nc.vector.scalar_tensor_tensor(ct[t][:], clev_rows(t), ku[:, t : t + 1], trt_sb[:, t, :], ALU.mult, ALU.mult)
+            nc.vector.scalar_tensor_tensor(ct[t][:], row(clev, t), ku[:, t : t + 1], trt_sb[:, t, :], ALU.mult, ALU.mult)
 
-        stage(("w1", 0))
-        round_on_scalar(("w1", 0), 0, P)
-        quantize(("w1", 0), 0, PACK)
-        for t in range(PACK):
-            product_pass(neg_m0[t], "w1", 0, t, True, False)
+        prepare(("w1", 0), ("stage1", "stage0"), neg_m0, lambda t: True, False)
 
-        first = [clev_steps(clev[0][:, t, :], up[0][:, t, :], down[0][:, t, :], trt_sb[:, t, :]) for t in range(2)]
+        first = [clev_steps(row(clev, t), row(up, t), row(down, t), trt_sb[:, t, :]) for t in range(2)]
         for k in range(3):
             first[0][k]()
             first[1][k]()
 
-        stage(("w1", 1))
-        round_on_scalar(("w1", 1), 0, P)
-        for t in range(PACK):
-            quantize(("w1", 1), t, t + 1)
-            product_pass(neg_m0[t], "w1", 1, t, False, True)
+        prepare(("w1", 1), ("up0", "down0"), neg_m0, lambda t: False, True)
         for t in range(PACK):
             if t != SPLIT_TILE:
                 product_pass(diff[t], "w1", 0, t, True, False)
@@ -186,73 +178,81 @@ def tile_picked_yuplif_dr_p_kernel(tc, x_words, x_scales, w1, w2, w3, trt, yy0, 
         make_ct(1)
         second[2]()
 
-        stage(("w2", 0))
-        round_on_scalar(("w2", 0), 0, P)
-        quantize(("w2", 0), 0, PACK)
-        for t in range(PACK):
-            product_pass(diff[t], "w2", 0, t, t == SPLIT_TILE, False)
-        stage(("w2", 1))
-        round_on_scalar(("w2", 1), 0, P)
+        prepare(("w2", 0), ("stage1", "stage0"), diff, lambda t: t == SPLIT_TILE, False)
         neg_m0_sb = sb("neg_m0_sb", [P, S], F32)
         nc.scalar.activation(neg_m0_sb[:], neg_m0[SPLIT_TILE][:], ACT.Copy)
-        for t in range(PACK):
-            quantize(("w2", 1), t, t + 1)
-            product_pass(diff[t], "w2", 1, t, False, True)
+        prepare(("w2", 1), ("up0", "down0"), diff, lambda t: False, True)
 
-        w4_grouped = sb("w4_grouped", [P, PACK * N], BF16, tag="down0")
+        w4_grouped = sb("w4_grouped", [P, PACK * N], BF16, tag="up1")
         nc.scalar.activation(
-            w4_grouped[:].rearrange("p (c i j) -> p c j i", i=4, j=PACK),
-            w4_raw[:].rearrange("p j (c i) -> p c j i", i=4),
+            w4_grouped[:].rearrange("p (c i j) -> p c j i", i=2, j=PACK),
+            w4_raw[:].rearrange("p j (c i) -> p c j i", i=2),
             ACT.Copy,
         )
         w4_codes = sb("w4_codes", [P, N], U32)
         w4_scales = sb("w4_scales", [P, N], U8)
-        nc.vector.quantize_mx(out=w4_codes[:].bitcast(FP8X4), scales=w4_scales[:], in_=w4_grouped[:])
 
         make_ct(2)
         make_ct(3)
         for t in range(PACK):
-            nc.vector.tensor_tensor(err[t][:], neg_m0[t][:], yy_sb[:, t, :], ALU.add)
-        for t in range(PACK):
-            nc.vector.scalar_tensor_tensor(ce[t][:], clev_rows(t), ku[:, t : t + 1], err[t][:], ALU.mult, ALU.mult)
-
+            nc.vector.tensor_tensor(row(err, t), neg_m0[t][:], yy_sb[:, t, :], ALU.add)
+        ce = [sb("ce%d" % g, [P, 2, S], F32, tag=("up0", "down0")[g]) for g in range(2)]
         diff_sb = sb("diff_sb", [P, S], F32)
-        nc.vector.tensor_tensor(diff_sb[:], diff[SPLIT_TILE][:], neg_m0_sb[:], ALU.add)
         dv = rows("dv")
         tau = sb("tau", [P, PACK, S], F32)
-        twin = [sb("twin%d" % h, [P, PACK, HALF], F32) for h in range(2)]
+        twin = [sb("twin%d" % q, [P, PACK, QUARTER], F32) for q in range(4)]
 
         def make_dv(t):
             d = diff_sb if t == SPLIT_TILE else diff[t]
             nc.vector.scalar_tensor_tensor(dv[t][:], ct[t][:], unit_sb[:, t : t + 1], d[:], ALU.subtract, ALU.mult)
 
-        make_dv(0)
-        for t in range(PACK):
-            if t + 1 < PACK:
-                make_dv(t + 1)
-            nc.vector.tensor_tensor(tau[:, t, :], ce[t][:], dv[t][:], ALU.subtract)
-            for h in range(2):
+        def make_ce(t):
+            nc.vector.tensor_tensor(row(ce, t), row(clev, t), row(err, t), ALU.mult)
+
+        def make_tau(t):
+            nc.vector.scalar_tensor_tensor(tau[:, t, :], row(ce, t), ku[:, t : t + 1], dv[t][:], ALU.mult, ALU.subtract)
+            for q in range(4):
                 nc.scalar.activation(
-                    twin[h][:, t, :],
-                    tau[:, t, :].indirect(tw_sb[:, h * HALF // 16 : (h + 1) * HALF // 16]),
+                    twin[q][:, t, :],
+                    tau[:, t, :].indirect(tw_sb[:, q * QUARTER // 16 : (q + 1) * QUARTER // 16]),
                     ACT.Copy,
                     scale=-0.5,
                 )
 
-        for h in range(2):
-            cols = slice(h * HALF, (h + 1) * HALF)
-            hid_grouped = sb("hid_grouped%d" % h, [P, PACK * HALF], BF16)
+        nc.vector.tensor_tensor(ce[0][:], clev[0][:], err[0][:], ALU.mult)
+        nc.vector.tensor_tensor(diff_sb[:], diff[SPLIT_TILE][:], neg_m0_sb[:], ALU.add)
+        make_dv(1)
+        make_dv(0)
+        make_tau(1)
+        make_ce(2)
+        make_tau(0)
+        make_dv(2)
+        make_ce(3)
+        make_tau(2)
+        make_dv(3)
+        nc.vector.quantize_mx(out=w4_codes[:].bitcast(FP8X4), scales=w4_scales[:], in_=w4_grouped[:])
+        make_tau(3)
+
+        chunks = [(0, HALF), (HALF, QUARTER), (HALF + QUARTER, QUARTER)]
+        hid_grouped = [sb("hid_grouped%d" % i, [P, PACK * w], BF16) for i, (c, w) in enumerate(chunks)]
+
+        def make_hid(i, c0):
+            c = chunks[i][0] + c0
             nc.vector.tensor_tensor(
-                hid_grouped[:].rearrange("p (c i t) -> p c t i", i=2, t=PACK),
-                tau[:, :, cols].rearrange("p t (c i) -> p c t i", i=2),
-                twin[h][:].rearrange("p t (c i) -> p c t i", i=2),
+                hid_grouped[i][:, PACK * c0 : PACK * (c0 + QUARTER)].rearrange("p (c i t) -> p c t i", i=2, t=PACK),
+                tau[:, :, c : c + QUARTER].rearrange("p t (c i) -> p c t i", i=2),
+                twin[c // QUARTER][:].rearrange("p t (c i) -> p c t i", i=2),
                 ALU.add,
             )
-            hid_codes = sb("hid_codes%d" % h, [P, HALF], U32)
-            hid_scales = sb("hid_scales%d" % h, [P, HALF], U8)
-            nc.vector.quantize_mx(out=hid_codes[:].bitcast(FP8X4), scales=hid_scales[:], in_=hid_grouped[:])
+
+        def finish(i):
+            c, w = chunks[i]
+            hid_codes = sb("hid_codes%d" % i, [P, w], U32)
+            hid_scales = sb("hid_scales%d" % i, [P, w], U8)
+            nc.vector.quantize_mx(out=hid_codes[:].bitcast(FP8X4), scales=hid_scales[:], in_=hid_grouped[i][:])
+            last = i == len(chunks) - 1
             for b in range(N // P):
-                acc = psum.tile([P, HALF], F32, name="acc%d%d" % (h, b), tag="b%d" % (2 * h + b))
+                acc = psum.tile([P, w], F32, name="acc%d%d" % (i, b), tag=("a%d" if last else "b%d") % ((2 * i + b) % PACK))
                 nc.tensor.matmul_mx(
                     out=acc[:],
                     lhsT=w4_codes[:, b * P : (b + 1) * P].bitcast(FP8X4),
@@ -262,9 +262,18 @@ def tile_picked_yuplif_dr_p_kernel(tc, x_words, x_scales, w1, w2, w3, trt, yy0, 
                     start=True,
                     stop=True,
                 )
-                res = sb("res%d%d" % (h, b), [P, HALF], F32)
-                if h == 1 and b == 1:
+                res = sb("res%d%d" % (i, b), [P, w], F32)
+                if last and b == 0:
                     nc.vector.tensor_copy(res[:], acc[:])
                 else:
                     nc.scalar.activation(res[:], acc[:], ACT.Copy)
-                nc.sync.dma_start(out=out[b * P : (b + 1) * P, cols], in_=res[:])
+                queue = nc.scalar if last and b == 1 else nc.sync
+                queue.dma_start(out=out[b * P : (b + 1) * P, c : c + w], in_=res[:])
+
+        make_hid(0, 0)
+        make_hid(0, QUARTER)
+        make_hid(1, 0)
+        finish(0)
+        make_hid(2, 0)
+        finish(1)
+        finish(2)

@@ -42,8 +42,8 @@ def tile_picked_yuplif_dr_p_kernel(tc, x_words, x_scales, w1, w2, w3, trt, yy0, 
         xs_table = sb("xs_table", [P, T], U8)
         raw = {(n, o): sb("raw_%s_%d" % (n, o), [P, PACK, H], F32) for n in ("w1", "w2", "w3") for o in range(PASSES)}
         w4_raw = sb("w4_raw", [P, PACK, N], F32)
-        trt_sb = sb("trt_sb", [P, PACK, S], F32)
-        yy_sb = sb("yy_sb", [P, PACK, S], F32)
+        trt_sb = [sb("trt_sb%d" % g, [P, 2, S], F32) for g in range(2)]
+        yy_sb = [sb("yy_sb%d" % g, [P, 2, S], F32) for g in range(2)]
         unit_sb = sb("unit_sb", [P, PACK], F32)
         weights = {"w1": w1, "w2": w2, "w3": w3}
 
@@ -54,59 +54,57 @@ def tile_picked_yuplif_dr_p_kernel(tc, x_words, x_scales, w1, w2, w3, trt, yy0, 
         def load_words(o):
             nc.sync.dma_start(out=x_table[o][:].bitcast(I32), in_=x_words[o].rearrange("p n r -> p (n r)").bitcast(I32))
 
+        def load_pair(tiles, src, g):
+            nc.sync.dma_start(out=tiles[g][:], in_=src.rearrange("(p t) j -> p t j", t=PACK)[:, 2 * g : 2 * g + 2, :])
+
         nc.gpsimd.memset(xs_table[:].bitcast(I32), 0)
         nc.sync.dma_start(out=offs_sb[:], in_=offs)
         load_words(0)
+        nc.scalar.dma_start(out=unit_sb[:], in_=unit.rearrange("(p t) o -> p (t o)", t=PACK))
         for q in range(4):
             nc.sync.dma_start(
                 out=xs_table[32 * q : 32 * q + 4 * PASSES, :].bitcast(I32),
                 in_=x_scales[:, 4 * q : 4 * q + 4, :].bitcast(I32),
             )
         load_weight("w3", 0)
-        load_words(1)
         load_weight("w3", 1)
-        nc.sync.dma_start(out=unit_sb[:], in_=unit.rearrange("(p t) o -> p (t o)", t=PACK))
-        nc.sync.dma_start(out=trt_sb[:], in_=trt.rearrange("(p t) j -> p t j", t=PACK))
+        load_words(1)
+        load_pair(trt_sb, trt, 0)
+        load_pair(trt_sb, trt, 1)
         load_weight("w1", 0)
         load_weight("w1", 1)
-        nc.sync.dma_start(out=tw_sb[:], in_=tw)
-        nc.sync.dma_start(out=yy_sb[:], in_=yy0.rearrange("(p t) j -> p t j", t=PACK))
         load_weight("w2", 0)
+        load_pair(yy_sb, yy0, 0)
         load_weight("w2", 1)
+        load_pair(yy_sb, yy0, 1)
         nc.sync.dma_start(out=w4_raw[:], in_=w4.rearrange("(p j) c -> p j c", j=PACK))
+        nc.sync.dma_start(out=tw_sb[:], in_=tw)
 
-        x_codes = [sb("x_codes%d" % o, [P, S], U32) for o in range(PASSES)]
+        x_codes = [sb("x_codes0", [P, S], U32)]
         x_sc = sb("x_sc", [P, S], U8)
         codes = {key: sb("codes_%s_%d" % key, [P, H], U32) for key in raw}
         scales = {key: sb("scales_%s_%d" % key, [P, H], U8) for key in raw}
-        grouped = {}
 
-        def round_pair(key, g, tag, engine="scalar"):
-            tile = sb("grp_%s_%d_%d" % (key + (g,)), [P, 2 * H], BF16, tag=tag)
-            grouped[key, g] = tile
-            dst = tile[:].rearrange("p (e m j) -> p m j e", e=2, j=PACK)
+        def round_pair(key, g, staging, engine="scalar"):
+            dst = staging.rearrange("p (e m j) -> p m j e", e=2, j=PACK)
             src = raw[key][:].rearrange("p j (m g e) -> p g m j e", g=2, e=2)[:, g]
             if engine == "vector":
                 nc.vector.tensor_copy(dst, src)
             else:
                 nc.scalar.activation(dst, src, ACT.Copy, scale=-1.0 if key[0] == "w1" else 1.0)
 
-        def quantize(key, t0, t1):
-            e0 = t0 % 2
-            nc.vector.quantize_mx(
-                out=codes[key][:, t0 * P : t1 * P].bitcast(FP8X4),
-                scales=scales[key][:, t0 * P : t1 * P],
-                in_=grouped[key, t0 // 2][:, e0 * H : (e0 + t1 - t0) * H],
-            )
+        def quantize(key, t0, staging):
+            cols = slice(t0 * P, t0 * P + staging.shape[1] // PACK)
+            nc.vector.quantize_mx(out=codes[key][:, cols].bitcast(FP8X4), scales=scales[key][:, cols], in_=staging)
 
-        def product_pass(acc, n, o, t, start, stop):
+        def product_pass(acc, n, o, t, start, stop, picked=slice(0, S)):
             cols = slice(t * P, (t + 1) * P)
             nc.tensor.matmul_mx(
                 out=acc[:],
                 lhsT=codes[n, o][:, cols].bitcast(FP8X4),
                 lhsT_scale=scales[n, o][:, cols],
-                rhs=x_codes[o][:].bitcast(FP8X4),
-                rhs_scale=x_sc[4 * o :, :],
+                rhs=x_codes[o][:, picked].bitcast(FP8X4),
+                rhs_scale=x_sc[4 * o :, picked],
                 start=start,
                 stop=stop,
             )
@@ -120,26 +118,56 @@ def tile_picked_yuplif_dr_p_kernel(tc, x_words, x_scales, w1, w2, w3, trt, yy0, 
         def row(tiles, t):
             return tiles[t // 2][:, t % 2, :]
 
-        def prepare(key, tags, acc, start, stop):
+        def staging_pair(key, g, tag):
+            return sb("grp_%s_%d_%d" % (key + (g,)), [P, 2 * H], BF16, tag=tag)[:]
+
+        def prepare_whole(key, tag, acc, start, stop):
+            staging = sb("grp_%s_%d" % key, [P, PACK * H], BF16, tag=tag)
             for g in range(2):
-                round_pair(key, g, tags[g])
-                quantize(key, 2 * g, 2 * g + 2)
-                for t in (2 * g, 2 * g + 1):
-                    product_pass(acc[t], key[0], key[1], t, start(t), stop)
+                round_pair(key, g, staging[:, 2 * g * H : 2 * (g + 1) * H])
+            quantize(key, 0, staging[:])
+            for t in range(PACK):
+                product_pass(acc[t], key[0], key[1], t, start(t), stop)
 
         nc.vector.tensor_copy(x_codes[0][:], x_table[0][:].indirect(offs_sb[:]))
         nc.vector.tensor_copy(x_sc[:], xs_table[:].indirect(offs_sb[:]))
-        nc.vector.tensor_copy(x_codes[1][:], x_table[1][:].indirect(offs_sb[:]))
-        pe = [psum.tile([P, S], F32, name="pe%d" % t, tag="a%d" % t) for t in range(PACK)]
-        prepare(("w3", 0), ("stage0", "stage1"), pe, lambda t: True, False)
-        round_pair(("w3", 1), 0, "stage0", "vector")
-        round_pair(("w3", 1), 1, "stage1")
-        up, down = pairs("up"), pairs("down")
-        for t in range(PACK):
-            quantize(("w3", 1), t, t + 1)
+        halves = [slice(0, HALF), slice(HALF, S)]
+        pe_first = [psum.tile([P, HALF], F32, name="pe_first%d" % h, tag=("a0", "b0")[h]) for h in range(2)]
+        pe = {t: psum.tile([P, S], F32, name="pe%d" % t, tag="a%d" % t) for t in range(1, PACK)}
+        staged = [staging_pair(("w3", 0), g, "stage%d" % g) for g in range(2)]
+        round_pair(("w3", 0), 0, staged[0], "vector")
+        round_pair(("w3", 0), 1, staged[1])
+        quantize(("w3", 0), 0, staged[0])
+        quantize(("w3", 0), 2, staged[1])
+        for h in range(2):
+            product_pass(pe_first[h], "w3", 0, 0, True, False, halves[h])
+        for t in range(1, PACK):
+            product_pass(pe[t], "w3", 0, t, True, False)
+        staged = [staging_pair(("w3", 1), g, "stage%d" % g) for g in range(2)]
+        round_pair(("w3", 1), 0, staged[0], "vector")
+        round_pair(("w3", 1), 1, staged[1])
+        quantize(("w3", 1), 0, staged[0])
+        x_codes.append(sb("x_codes1", [P, S], U32, tag="stage0"))
+        up_first = [sb("up_first%d" % h, [P, HALF], F32) for h in range(2)]
+        down_first = [sb("down_first%d" % h, [P, HALF], F32) for h in range(2)]
+        up = [sb("up0", [P, S], F32), sb("up1", [P, 2, S], F32)]
+        down = [sb("down0", [P, S], F32), sb("down1", [P, 2, S], F32)]
+
+        def tanh_pair(hi, lo, acc):
+            nc.scalar.activation(hi, acc[:], ACT.Tanh, bias=LN3, scale=0.5)
+            nc.scalar.activation(lo, acc[:], ACT.Tanh, bias=-LN3, scale=0.5)
+
+        for h in range(2):
+            listed = offs_sb[:, h * HALF // 16 : (h + 1) * HALF // 16]
+            nc.vector.tensor_copy(x_codes[1][:, halves[h]], x_table[1][:].indirect(listed))
+            product_pass(pe_first[h], "w3", 1, 0, False, True, halves[h])
+            tanh_pair(up_first[h][:], down_first[h][:], pe_first[h])
+        product_pass(pe[1], "w3", 1, 1, False, True)
+        tanh_pair(up[0][:], down[0][:], pe[1])
+        quantize(("w3", 1), 2, staged[1])
+        for t in (2, 3):
             product_pass(pe[t], "w3", 1, t, False, True)
-            nc.scalar.activation(row(up, t), pe[t][:], ACT.Tanh, bias=LN3, scale=0.5)
-            nc.scalar.activation(row(down, t), pe[t][:], ACT.Tanh, bias=-LN3, scale=0.5)
+            tanh_pair(row(up, t), row(down, t), pe[t])
 
         neg_m0 = [psum.tile([P, S], F32, name="neg_m0%d" % t, tag="b%d" % t) for t in range(PACK)]
         diff = [psum.tile([P, S], F32, name="diff%d" % t, tag="a%d" % t) for t in range(PACK)]
@@ -156,32 +184,45 @@ def tile_picked_yuplif_dr_p_kernel(tc, x_words, x_scales, w1, w2, w3, trt, yy0, 
             ]
 
         def make_ct(t):
-            nc.vector.scalar_tensor_tensor(ct[t][:], row(clev, t), ku[:, t : t + 1], trt_sb[:, t, :], ALU.mult, ALU.mult)
+            nc.vector.scalar_tensor_tensor(ct[t][:], row(clev, t), ku[:, t : t + 1], row(trt_sb, t), ALU.mult, ALU.mult)
 
-        prepare(("w1", 0), ("stage1", "stage0"), neg_m0, lambda t: True, False)
+        first = [
+            clev_steps(clev[0][:, 0, halves[h]], up_first[h][:], down_first[h][:], trt_sb[0][:, 0, halves[h]]) for h in range(2)
+        ]
+        first.append(clev_steps(row(clev, 1), up[0][:], down[0][:], row(trt_sb, 1)))
+        first[0][0]()
+        first[0][1]()
+        first[1][0]()
+        first[0][2]()
+        first[1][1]()
+        prepare_whole(("w1", 0), "up_first0", neg_m0, lambda t: True, False)
+        first[2][0]()
+        first[1][2]()
+        first[2][1]()
+        make_ct(0)
+        first[2][2]()
 
-        first = [clev_steps(row(clev, t), row(up, t), row(down, t), trt_sb[:, t, :]) for t in range(2)]
-        for k in range(3):
-            first[0][k]()
-            first[1][k]()
-
-        prepare(("w1", 1), ("up0", "down0"), neg_m0, lambda t: False, True)
+        prepare_whole(("w1", 1), "up0", neg_m0, lambda t: False, True)
         for t in range(PACK):
             if t != SPLIT_TILE:
                 product_pass(diff[t], "w1", 0, t, True, False)
                 product_pass(diff[t], "w1", 1, t, False, False)
 
-        second = clev_steps(clev[1][:], up[1][:], down[1][:], trt_sb[:, 2:4, :])
+        second = clev_steps(clev[1][:], up[1][:], down[1][:], trt_sb[1][:])
         second[0]()
-        make_ct(0)
-        second[1]()
         make_ct(1)
+        second[1]()
         second[2]()
 
-        prepare(("w2", 0), ("stage1", "stage0"), diff, lambda t: t == SPLIT_TILE, False)
+        prepare_whole(("w2", 0), "up_first0", diff, lambda t: t == SPLIT_TILE, False)
         neg_m0_sb = sb("neg_m0_sb", [P, S], F32)
+        for g in range(2):
+            staging = staging_pair(("w2", 1), g, ("up0", "down0")[g])
+            round_pair(("w2", 1), g, staging)
+            quantize(("w2", 1), 2 * g, staging)
+            for t in (2 * g, 2 * g + 1):
+                product_pass(diff[t], "w2", 1, t, False, True)
         nc.scalar.activation(neg_m0_sb[:], neg_m0[SPLIT_TILE][:], ACT.Copy)
-        prepare(("w2", 1), ("up0", "down0"), diff, lambda t: False, True)
 
         w4_grouped = sb("w4_grouped", [P, PACK * N], BF16, tag="up1")
         nc.scalar.activation(
@@ -195,7 +236,7 @@ def tile_picked_yuplif_dr_p_kernel(tc, x_words, x_scales, w1, w2, w3, trt, yy0, 
         make_ct(2)
         make_ct(3)
         for t in range(PACK):
-            nc.vector.tensor_tensor(row(err, t), neg_m0[t][:], yy_sb[:, t, :], ALU.add)
+            nc.vector.tensor_tensor(row(err, t), neg_m0[t][:], row(yy_sb, t), ALU.add)
         ce = [sb("ce%d" % g, [P, 2, S], F32, tag=("up0", "down0")[g]) for g in range(2)]
         diff_sb = sb("diff_sb", [P, S], F32)
         dv = rows("dv")

@@ -74,8 +74,8 @@ def tile_picked_yuplif_dr_p_kernel(tc, x_words, x_scales, w1, w2, w3, trt, yy0, 
         load_weight("w1", 0)
         load_weight("w1", 1)
         load_weight("w2", 0)
-        load_pair(yy_sb, yy0, 0)
         load_weight("w2", 1)
+        load_pair(yy_sb, yy0, 0)
         load_pair(yy_sb, yy0, 1)
         nc.sync.dma_start(out=w4_raw[:], in_=w4.rearrange("(p j) c -> p j c", j=PACK))
         nc.sync.dma_start(out=tw_sb[:], in_=tw)
@@ -121,10 +121,10 @@ def tile_picked_yuplif_dr_p_kernel(tc, x_words, x_scales, w1, w2, w3, trt, yy0, 
         def staging_pair(key, g, tag):
             return sb("grp_%s_%d_%d" % (key + (g,)), [P, 2 * H], BF16, tag=tag)[:]
 
-        def prepare_whole(key, tag, acc, start, stop):
+        def prepare_whole(key, tag, acc, start, stop, engines=("scalar", "scalar")):
             staging = sb("grp_%s_%d" % key, [P, PACK * H], BF16, tag=tag)
             for g in range(2):
-                round_pair(key, g, staging[:, 2 * g * H : 2 * (g + 1) * H])
+                round_pair(key, g, staging[:, 2 * g * H : 2 * (g + 1) * H], engines[g])
             quantize(key, 0, staging[:])
             for t in range(PACK):
                 product_pass(acc[t], key[0], key[1], t, start(t), stop)
@@ -173,7 +173,7 @@ def tile_picked_yuplif_dr_p_kernel(tc, x_words, x_scales, w1, w2, w3, trt, yy0, 
         diff = [psum.tile([P, S], F32, name="diff%d" % t, tag="a%d" % t) for t in range(PACK)]
         ku = sb("ku", [P, PACK], F32)
         nc.vector.tensor_scalar(ku[:], unit_sb[:], KAPPA, None, ALU.mult)
-        clev, err = pairs("clev"), pairs("err")
+        clev = pairs("clev")
         ct = rows("ct")
 
         def clev_steps(dst, hi, lo, treat):
@@ -196,6 +196,9 @@ def tile_picked_yuplif_dr_p_kernel(tc, x_words, x_scales, w1, w2, w3, trt, yy0, 
         first[0][2]()
         first[1][1]()
         prepare_whole(("w1", 0), "up_first0", neg_m0, lambda t: True, False)
+        for t in range(PACK):
+            if t != SPLIT_TILE:
+                product_pass(diff[t], "w1", 0, t, True, False)
         first[2][0]()
         first[1][2]()
         first[2][1]()
@@ -205,7 +208,6 @@ def tile_picked_yuplif_dr_p_kernel(tc, x_words, x_scales, w1, w2, w3, trt, yy0, 
         prepare_whole(("w1", 1), "up0", neg_m0, lambda t: False, True)
         for t in range(PACK):
             if t != SPLIT_TILE:
-                product_pass(diff[t], "w1", 0, t, True, False)
                 product_pass(diff[t], "w1", 1, t, False, False)
 
         second = clev_steps(clev[1][:], up[1][:], down[1][:], trt_sb[1][:])
@@ -214,17 +216,16 @@ def tile_picked_yuplif_dr_p_kernel(tc, x_words, x_scales, w1, w2, w3, trt, yy0, 
         second[1]()
         second[2]()
 
-        prepare_whole(("w2", 0), "up_first0", diff, lambda t: t == SPLIT_TILE, False)
-        neg_m0_sb = sb("neg_m0_sb", [P, S], F32)
-        for g in range(2):
-            staging = staging_pair(("w2", 1), g, ("up0", "down0")[g])
-            round_pair(("w2", 1), g, staging)
-            quantize(("w2", 1), 2 * g, staging)
-            for t in (2 * g, 2 * g + 1):
-                product_pass(diff[t], "w2", 1, t, False, True)
-        nc.scalar.activation(neg_m0_sb[:], neg_m0[SPLIT_TILE][:], ACT.Copy)
+        prepare_whole(("w2", 0), "up_first0", diff, lambda t: t == SPLIT_TILE, False, ("scalar", "vector"))
+        neg_m0_sb = sb("neg_m0_sb", [P, S], F32, tag="raw_w2_1")
+        staged = [staging_pair(("w2", 1), g, ("down0", "down1")[g]) for g in range(2)]
+        round_pair(("w2", 1), 0, staged[0])
+        quantize(("w2", 1), 0, staged[0])
+        for t in (1, 0):
+            product_pass(diff[t], "w2", 1, t, False, True)
+        round_pair(("w2", 1), 1, staged[1])
 
-        w4_grouped = sb("w4_grouped", [P, PACK * N], BF16, tag="up1")
+        w4_grouped = sb("w4_grouped", [P, PACK * N], BF16, tag="raw_w2_0")
         nc.scalar.activation(
             w4_grouped[:].rearrange("p (c i j) -> p c j i", i=2, j=PACK),
             w4_raw[:].rearrange("p j (c i) -> p c j i", i=2),
@@ -235,34 +236,49 @@ def tile_picked_yuplif_dr_p_kernel(tc, x_words, x_scales, w1, w2, w3, trt, yy0, 
 
         make_ct(2)
         make_ct(3)
-        for t in range(PACK):
-            nc.vector.tensor_tensor(row(err, t), neg_m0[t][:], row(yy_sb, t), ALU.add)
-        ce = [sb("ce%d" % g, [P, 2, S], F32, tag=("up0", "down0")[g]) for g in range(2)]
+        err = sb("err", [P, PACK, S], F32, tag="down0")
+        ce = pairs("ce")
+        for t in (1, 0, 2, 3):
+            nc.vector.tensor_tensor(err[:, t, :], neg_m0[t][:], row(yy_sb, t), ALU.add)
+        nc.scalar.activation(neg_m0_sb[:], neg_m0[SPLIT_TILE][:], ACT.Copy)
+        for t in (1, 0):
+            nc.gpsimd.tensor_tensor(row(ce, t), row(clev, t), err[:, t, :], ALU.mult)
         diff_sb = sb("diff_sb", [P, S], F32)
         dv = rows("dv")
         tau = sb("tau", [P, PACK, S], F32)
-        twin = [sb("twin%d" % q, [P, PACK, QUARTER], F32) for q in range(4)]
+        twin = [sb("twin%d" % h, [P, PACK, HALF], F32) for h in range(2)]
 
         def make_dv(t):
             d = diff_sb if t == SPLIT_TILE else diff[t]
             nc.vector.scalar_tensor_tensor(dv[t][:], ct[t][:], unit_sb[:, t : t + 1], d[:], ALU.subtract, ALU.mult)
 
         def make_ce(t):
-            nc.vector.tensor_tensor(row(ce, t), row(clev, t), row(err, t), ALU.mult)
+            nc.vector.tensor_tensor(row(ce, t), row(clev, t), err[:, t, :], ALU.mult)
 
-        def make_tau(t):
+        def make_tau(t, step=HALF):
             nc.vector.scalar_tensor_tensor(tau[:, t, :], row(ce, t), ku[:, t : t + 1], dv[t][:], ALU.mult, ALU.subtract)
-            for q in range(4):
+            for c in range(0, S, step):
                 nc.scalar.activation(
-                    twin[q][:, t, :],
-                    tau[:, t, :].indirect(tw_sb[:, q * QUARTER // 16 : (q + 1) * QUARTER // 16]),
+                    twin[c // HALF][:, t, c % HALF : c % HALF + step],
+                    tau[:, t, :].indirect(tw_sb[:, c // 16 : (c + step) // 16]),
                     ACT.Copy,
                     scale=-0.5,
                 )
 
-        nc.vector.tensor_tensor(ce[0][:], clev[0][:], err[0][:], ALU.mult)
-        nc.vector.tensor_tensor(diff_sb[:], diff[SPLIT_TILE][:], neg_m0_sb[:], ALU.add)
         make_dv(1)
+        nc.vector.tensor_tensor(diff_sb[:], diff[SPLIT_TILE][:], neg_m0_sb[:], ALU.add)
+        late_codes = sb("late_codes", [P, 2 * P], U32, tag="raw_w2_1")
+        nc.vector.quantize_mx(out=late_codes[:].bitcast(FP8X4), scales=scales["w2", 1][:, 2 * P :], in_=staged[1])
+        for t in (2, 3):
+            nc.tensor.matmul_mx(
+                out=diff[t][:],
+                lhsT=late_codes[:, (t - 2) * P : (t - 1) * P].bitcast(FP8X4),
+                lhsT_scale=scales["w2", 1][:, t * P : (t + 1) * P],
+                rhs=x_codes[1][:].bitcast(FP8X4),
+                rhs_scale=x_sc[4:, :],
+                start=False,
+                stop=True,
+            )
         make_dv(0)
         make_tau(1)
         make_ce(2)
@@ -272,7 +288,7 @@ def tile_picked_yuplif_dr_p_kernel(tc, x_words, x_scales, w1, w2, w3, trt, yy0, 
         make_tau(2)
         make_dv(3)
         nc.vector.quantize_mx(out=w4_codes[:].bitcast(FP8X4), scales=w4_scales[:], in_=w4_grouped[:])
-        make_tau(3)
+        make_tau(3, QUARTER)
 
         chunks = [(0, HALF), (HALF, QUARTER), (HALF + QUARTER, QUARTER)]
         hid_grouped = [sb("hid_grouped%d" % i, [P, PACK * w], BF16) for i, (c, w) in enumerate(chunks)]
@@ -282,7 +298,7 @@ def tile_picked_yuplif_dr_p_kernel(tc, x_words, x_scales, w1, w2, w3, trt, yy0, 
             nc.vector.tensor_tensor(
                 hid_grouped[i][:, PACK * c0 : PACK * (c0 + QUARTER)].rearrange("p (c i t) -> p c t i", i=2, t=PACK),
                 tau[:, :, c : c + QUARTER].rearrange("p t (c i) -> p c t i", i=2),
-                twin[c // QUARTER][:].rearrange("p t (c i) -> p c t i", i=2),
+                twin[c // HALF][:, :, c % HALF : c % HALF + QUARTER].rearrange("p t (c i) -> p c t i", i=2),
                 ALU.add,
             )
 

import math
from contextlib import ExitStack

import concourse.mybir as mybir

K, T, S, N, H = 1024, 1024, 512, 256, 512
FLOPS = 3 * 2 * K * H * S + 2 * H * N * S

F32 = mybir.dt.float32
BF16 = mybir.dt.bfloat16
I32 = mybir.dt.int32
U32 = mybir.dt.uint32
U16 = mybir.dt.uint16
U8 = mybir.dt.uint8
FP8X4 = mybir.dt.float8_e4m3fn_x4
ALU = mybir.AluOpType
ACT = mybir.ActivationFunctionType

P = 128
PACK = 4
PASSES = K // (P * PACK)
HALF = S // 2
QUARTER = S // 4
LN3 = math.log(3.0)
ALPHA = 1.25
KAPPA = -0.3 * 40.0 / 9.0
SPLIT_TILE = 0


def tile_picked_yuplif_dr_p_kernel(tc, x_words, x_scales, w1, w2, w3, trt, yy0, unit, w4, offs, tw, out):
    nc = tc.nc
    with ExitStack() as ctx:
        keep = ctx.enter_context(tc.tile_pool(name="keep", bufs=1))
        psum = ctx.enter_context(tc.psum_pool(name="psum", bufs=1))

        def sb(name, shape, dtype, tag=None):
            return keep.tile(shape, dtype, name=name, tag=tag or name, align_bytes=64)

        offs_sb = keep.tile([P, S // 16], U16, name="offs_sb")
        tw_sb = keep.tile([P, S // 16], U16, name="tw_sb")
        x_table = [sb("x_table%d" % o, [P, T], U32) for o in range(PASSES)]
        xs_table = sb("xs_table", [P, T], U8)
        raw = {(n, o): sb("raw_%s_%d" % (n, o), [P, PACK, H], F32) for n in ("w1", "w2", "w3") for o in range(PASSES)}
        w4_raw = sb("w4_raw", [P, PACK, N], F32)
        trt_sb = [sb("trt_sb%d" % g, [P, 2, S], F32) for g in range(2)]
        yy_sb = [sb("yy_sb%d" % g, [P, 2, S], F32) for g in range(2)]
        unit_sb = sb("unit_sb", [P, PACK], F32)
        weights = {"w1": w1, "w2": w2, "w3": w3}

        def load_weight(n, o):
            rows = weights[n][o * P * PACK : (o + 1) * P * PACK, :]
            nc.sync.dma_start(out=raw[n, o][:], in_=rows.rearrange("(p j) c -> p j c", j=PACK))

        def load_words(o):
            nc.sync.dma_start(out=x_table[o][:].bitcast(I32), in_=x_words[o].rearrange("p n r -> p (n r)").bitcast(I32))

        def load_pair(tiles, src, g):
            nc.sync.dma_start(out=tiles[g][:], in_=src.rearrange("(p t) j -> p t j", t=PACK)[:, 2 * g : 2 * g + 2, :])

        nc.gpsimd.memset(xs_table[:].bitcast(I32), 0)
        nc.sync.dma_start(out=offs_sb[:], in_=offs)
        load_words(0)
        nc.scalar.dma_start(out=unit_sb[:], in_=unit.rearrange("(p t) o -> p (t o)", t=PACK))
        for q in range(4):
            nc.sync.dma_start(
                out=xs_table[32 * q : 32 * q + 4 * PASSES, :].bitcast(I32),
                in_=x_scales[:, 4 * q : 4 * q + 4, :].bitcast(I32),
            )
        load_weight("w3", 0)
        load_weight("w3", 1)
        load_words(1)
        load_pair(trt_sb, trt, 0)
        load_pair(trt_sb, trt, 1)
        load_weight("w1", 0)
        load_weight("w1", 1)
        load_weight("w2", 0)
        load_weight("w2", 1)
        load_pair(yy_sb, yy0, 0)
        load_pair(yy_sb, yy0, 1)
        nc.sync.dma_start(out=w4_raw[:], in_=w4.rearrange("(p j) c -> p j c", j=PACK))
        nc.sync.dma_start(out=tw_sb[:], in_=tw)

        x_codes = [sb("x_codes0", [P, S], U32)]
        x_sc = sb("x_sc", [P, S], U8)
        codes = {key: sb("codes_%s_%d" % key, [P, H], U32) for key in raw}
        scales = {key: sb("scales_%s_%d" % key, [P, H], U8) for key in raw}

        def round_pair(key, g, staging, engine="scalar"):
            dst = staging.rearrange("p (e m j) -> p m j e", e=2, j=PACK)
            src = raw[key][:].rearrange("p j (m g e) -> p g m j e", g=2, e=2)[:, g]
            if engine == "vector":
                nc.vector.tensor_copy(dst, src)
            else:
                nc.scalar.activation(dst, src, ACT.Copy, scale=-1.0 if key[0] == "w1" else 1.0)

        def quantize(key, t0, staging):
            cols = slice(t0 * P, t0 * P + staging.shape[1] // PACK)
            nc.vector.quantize_mx(out=codes[key][:, cols].bitcast(FP8X4), scales=scales[key][:, cols], in_=staging)

        def product_pass(acc, n, o, t, start, stop, picked=slice(0, S)):
            cols = slice(t * P, (t + 1) * P)
            nc.tensor.matmul_mx(
                out=acc[:],
                lhsT=codes[n, o][:, cols].bitcast(FP8X4),
                lhsT_scale=scales[n, o][:, cols],
                rhs=x_codes[o][:, picked].bitcast(FP8X4),
                rhs_scale=x_sc[4 * o :, picked],
                start=start,
                stop=stop,
            )

        def rows(name):
            return [sb("%s%d" % (name, t), [P, S], F32) for t in range(PACK)]

        def pairs(name):
            return [sb("%s%d" % (name, g), [P, 2, S], F32) for g in range(2)]

        def row(tiles, t):
            return tiles[t // 2][:, t % 2, :]

        def staging_pair(key, g, tag):
            return sb("grp_%s_%d_%d" % (key + (g,)), [P, 2 * H], BF16, tag=tag)[:]

        def prepare_whole(key, tag, acc, start, stop, engines=("scalar", "scalar")):
            staging = sb("grp_%s_%d" % key, [P, PACK * H], BF16, tag=tag)
            for g in range(2):
                round_pair(key, g, staging[:, 2 * g * H : 2 * (g + 1) * H], engines[g])
            quantize(key, 0, staging[:])
            for t in range(PACK):
                product_pass(acc[t], key[0], key[1], t, start(t), stop)

        nc.vector.tensor_copy(x_codes[0][:], x_table[0][:].indirect(offs_sb[:]))
        nc.vector.tensor_copy(x_sc[:], xs_table[:].indirect(offs_sb[:]))
        halves = [slice(0, HALF), slice(HALF, S)]
        pe_first = [psum.tile([P, HALF], F32, name="pe_first%d" % h, tag=("a0", "b0")[h]) for h in range(2)]
        pe = {t: psum.tile([P, S], F32, name="pe%d" % t, tag="a%d" % t) for t in range(1, PACK)}
        staged = [staging_pair(("w3", 0), g, "stage%d" % g) for g in range(2)]
        round_pair(("w3", 0), 0, staged[0], "vector")
        round_pair(("w3", 0), 1, staged[1])
        quantize(("w3", 0), 0, staged[0])
        quantize(("w3", 0), 2, staged[1])
        for h in range(2):
            product_pass(pe_first[h], "w3", 0, 0, True, False, halves[h])
        for t in range(1, PACK):
            product_pass(pe[t], "w3", 0, t, True, False)
        staged = [staging_pair(("w3", 1), g, "stage%d" % g) for g in range(2)]
        round_pair(("w3", 1), 0, staged[0], "vector")
        round_pair(("w3", 1), 1, staged[1])
        quantize(("w3", 1), 0, staged[0])
        x_codes.append(sb("x_codes1", [P, S], U32, tag="stage0"))
        up_first = [sb("up_first%d" % h, [P, HALF], F32) for h in range(2)]
        down_first = [sb("down_first%d" % h, [P, HALF], F32) for h in range(2)]
        up = [sb("up0", [P, S], F32), sb("up1", [P, 2, S], F32)]
        down = [sb("down0", [P, S], F32), sb("down1", [P, 2, S], F32)]

        def tanh_pair(hi, lo, acc):
            nc.scalar.activation(hi, acc[:], ACT.Tanh, bias=LN3, scale=0.5)
            nc.scalar.activation(lo, acc[:], ACT.Tanh, bias=-LN3, scale=0.5)

        for h in range(2):
            listed = offs_sb[:, h * HALF // 16 : (h + 1) * HALF // 16]
            nc.vector.tensor_copy(x_codes[1][:, halves[h]], x_table[1][:].indirect(listed))
            product_pass(pe_first[h], "w3", 1, 0, False, True, halves[h])
            tanh_pair(up_first[h][:], down_first[h][:], pe_first[h])
        product_pass(pe[1], "w3", 1, 1, False, True)
        tanh_pair(up[0][:], down[0][:], pe[1])
        quantize(("w3", 1), 2, staged[1])
        for t in (2, 3):
            product_pass(pe[t], "w3", 1, t, False, True)
            tanh_pair(row(up, t), row(down, t), pe[t])

        neg_m0 = [psum.tile([P, S], F32, name="neg_m0%d" % t, tag="b%d" % t) for t in range(PACK)]
        diff = [psum.tile([P, S], F32, name="diff%d" % t, tag="a%d" % t) for t in range(PACK)]
        ku = sb("ku", [P, PACK], F32)
        nc.vector.tensor_scalar(ku[:], unit_sb[:], KAPPA, None, ALU.mult)
        clev = pairs("clev")
        ct = rows("ct")

        def clev_steps(dst, hi, lo, treat):
            return [
                lambda: nc.vector.tensor_tensor(hi, hi, lo, ALU.subtract),
                lambda: nc.vector.scalar_tensor_tensor(hi, hi, -2.0 * ALPHA, treat, ALU.add, ALU.mult),
                lambda: nc.vector.scalar_tensor_tensor(dst, lo, ALPHA, hi, ALU.add, ALU.add),
            ]

        def make_ct(t):
            nc.vector.scalar_tensor_tensor(ct[t][:], row(clev, t), ku[:, t : t + 1], row(trt_sb, t), ALU.mult, ALU.mult)

        first = [
            clev_steps(clev[0][:, 0, halves[h]], up_first[h][:], down_first[h][:], trt_sb[0][:, 0, halves[h]]) for h in range(2)
        ]
        first.append(clev_steps(row(clev, 1), up[0][:], down[0][:], row(trt_sb, 1)))
        first[0][0]()
        first[0][1]()
        first[1][0]()
        first[0][2]()
        first[1][1]()
        prepare_whole(("w1", 0), "up_first0", neg_m0, lambda t: True, False)
        for t in range(PACK):
            if t != SPLIT_TILE:
                product_pass(diff[t], "w1", 0, t, True, False)
        first[2][0]()
        first[1][2]()
        first[2][1]()
        make_ct(0)
        first[2][2]()

        prepare_whole(("w1", 1), "up0", neg_m0, lambda t: False, True)
        for t in range(PACK):
            if t != SPLIT_TILE:
                product_pass(diff[t], "w1", 1, t, False, False)

        second = clev_steps(clev[1][:], up[1][:], down[1][:], trt_sb[1][:])
        second[0]()
        make_ct(1)
        second[1]()
        second[2]()

        prepare_whole(("w2", 0), "up_first0", diff, lambda t: t == SPLIT_TILE, False, ("scalar", "vector"))
        neg_m0_sb = sb("neg_m0_sb", [P, S], F32, tag="raw_w2_1")
        staged = [staging_pair(("w2", 1), g, ("down0", "down1")[g]) for g in range(2)]
        round_pair(("w2", 1), 0, staged[0])
        quantize(("w2", 1), 0, staged[0])
        for t in (1, 0):
            product_pass(diff[t], "w2", 1, t, False, True)
        round_pair(("w2", 1), 1, staged[1])

        w4_grouped = sb("w4_grouped", [P, PACK * N], BF16, tag="raw_w2_0")
        nc.scalar.activation(
            w4_grouped[:].rearrange("p (c i j) -> p c j i", i=2, j=PACK),
            w4_raw[:].rearrange("p j (c i) -> p c j i", i=2),
            ACT.Copy,
        )
        w4_codes = sb("w4_codes", [P, N], U32)
        w4_scales = sb("w4_scales", [P, N], U8)

        make_ct(2)
        make_ct(3)
        err = sb("err", [P, PACK, S], F32, tag="down0")
        ce = pairs("ce")
        for t in (1, 0, 2, 3):
            nc.vector.tensor_tensor(err[:, t, :], neg_m0[t][:], row(yy_sb, t), ALU.add)
        nc.scalar.activation(neg_m0_sb[:], neg_m0[SPLIT_TILE][:], ACT.Copy)
        for t in (1, 0):
            nc.gpsimd.tensor_tensor(row(ce, t), row(clev, t), err[:, t, :], ALU.mult)
        diff_sb = sb("diff_sb", [P, S], F32)
        dv = rows("dv")
        tau = sb("tau", [P, PACK, S], F32)
        twin = [sb("twin%d" % h, [P, PACK, HALF], F32) for h in range(2)]

        def make_dv(t):
            d = diff_sb if t == SPLIT_TILE else diff[t]
            nc.vector.scalar_tensor_tensor(dv[t][:], ct[t][:], unit_sb[:, t : t + 1], d[:], ALU.subtract, ALU.mult)

        def make_ce(t):
            nc.vector.tensor_tensor(row(ce, t), row(clev, t), err[:, t, :], ALU.mult)

        def make_tau(t, step=HALF):
            nc.vector.scalar_tensor_tensor(tau[:, t, :], row(ce, t), ku[:, t : t + 1], dv[t][:], ALU.mult, ALU.subtract)
            for c in range(0, S, step):
                nc.scalar.activation(
                    twin[c // HALF][:, t, c % HALF : c % HALF + step],
                    tau[:, t, :].indirect(tw_sb[:, c // 16 : (c + step) // 16]),
                    ACT.Copy,
                    scale=-0.5,
                )

        make_dv(1)
        nc.vector.tensor_tensor(diff_sb[:], diff[SPLIT_TILE][:], neg_m0_sb[:], ALU.add)
        late_codes = sb("late_codes", [P, 2 * P], U32, tag="raw_w2_1")
        nc.vector.quantize_mx(out=late_codes[:].bitcast(FP8X4), scales=scales["w2", 1][:, 2 * P :], in_=staged[1])
        for t in (2, 3):
            nc.tensor.matmul_mx(
                out=diff[t][:],
                lhsT=late_codes[:, (t - 2) * P : (t - 1) * P].bitcast(FP8X4),
                lhsT_scale=scales["w2", 1][:, t * P : (t + 1) * P],
                rhs=x_codes[1][:].bitcast(FP8X4),
                rhs_scale=x_sc[4:, :],
                start=False,
                stop=True,
            )
        make_dv(0)
        make_tau(1)
        make_ce(2)
        make_tau(0)
        make_dv(2)
        make_ce(3)
        make_tau(2)
        make_dv(3)
        nc.vector.quantize_mx(out=w4_codes[:].bitcast(FP8X4), scales=w4_scales[:], in_=w4_grouped[:])
        make_tau(3, QUARTER)

        chunks = [(0, HALF), (HALF, QUARTER), (HALF + QUARTER, QUARTER)]
        hid_grouped = [sb("hid_grouped%d" % i, [P, PACK * w], BF16) for i, (c, w) in enumerate(chunks)]

        def make_hid(i, c0):
            c = chunks[i][0] + c0
            nc.vector.tensor_tensor(
                hid_grouped[i][:, PACK * c0 : PACK * (c0 + QUARTER)].rearrange("p (c i t) -> p c t i", i=2, t=PACK),
                tau[:, :, c : c + QUARTER].rearrange("p t (c i) -> p c t i", i=2),
                twin[c // HALF][:, :, c % HALF : c % HALF + QUARTER].rearrange("p t (c i) -> p c t i", i=2),
                ALU.add,
            )

        def finish(i):
            c, w = chunks[i]
            hid_codes = sb("hid_codes%d" % i, [P, w], U32)
            hid_scales = sb("hid_scales%d" % i, [P, w], U8)
            nc.vector.quantize_mx(out=hid_codes[:].bitcast(FP8X4), scales=hid_scales[:], in_=hid_grouped[i][:])
            last = i == len(chunks) - 1
            for b in range(N // P):
                acc = psum.tile([P, w], F32, name="acc%d%d" % (i, b), tag=("a%d" if last else "b%d") % ((2 * i + b) % PACK))
                nc.tensor.matmul_mx(
                    out=acc[:],
                    lhsT=w4_codes[:, b * P : (b + 1) * P].bitcast(FP8X4),
                    lhsT_scale=w4_scales[:, b * P : (b + 1) * P],
                    rhs=hid_codes[:].bitcast(FP8X4),
                    rhs_scale=hid_scales[:],
                    start=True,
                    stop=True,
                )
                res = sb("res%d%d" % (i, b), [P, w], F32)
                if last and b == 0:
                    nc.vector.tensor_copy(res[:], acc[:])
                else:
                    nc.scalar.activation(res[:], acc[:], ACT.Copy)
                queue = nc.scalar if last and b == 1 else nc.sync
                queue.dma_start(out=out[b * P : (b + 1) * P, c : c + w], in_=res[:])

        make_hid(0, 0)
        make_hid(0, QUARTER)
        make_hid(1, 0)
        finish(0)
        make_hid(2, 0)
        finish(1)
        finish(2)
